import numpy as np
import ml_dtypes


def mxq(x, axis, fmt="e4m3"):
    dtype, down = {"e4m3": (ml_dtypes.float8_e4m3fn, 7), "e5m2": (ml_dtypes.float8_e5m2, 14)}[fmt]
    v = np.moveaxis(np.asarray(x, np.float32).astype(ml_dtypes.bfloat16).astype(np.float64), axis, -1)
    blocks = v.reshape(v.shape[:-1] + (-1, 32))
    amax = np.abs(blocks).max(-1, keepdims=True)
    byte = np.maximum(np.where(amax > 0, np.frexp(amax)[1] - 1 + 127, 0) - down, 1)
    scale = np.exp2(byte - 127.0)
    codes = (blocks / scale).astype(np.float32).astype(dtype).astype(np.float64)
    return np.moveaxis((codes * scale).reshape(v.shape), -1, axis)


WIDE = False


def mx_kscale(k):
    if not WIDE:
        return np.ones(k)
    levels = np.array([10, -10, 5, -5, 0])
    if k % 512:
        return np.exp2(np.random.permutation(np.resize(levels, k // 32))).repeat(32)
    a = np.empty((k // 512, 16))
    for p in range(k // 512):
        a[p, :8] = np.random.permutation(np.resize(levels, 8))
        for g in range(8):
            far = levels[np.abs(levels - a[p, g]) >= 10]
            a[p, g + 8] = far[np.random.randint(len(far))]
    return np.exp2(a.ravel()).repeat(32)


def f64(x):
    return np.asarray(x).astype(np.float64)


def striped8(idx):
    return np.asarray(idx).reshape(8, -1, 16).transpose(0, 2, 1).reshape(128, -1).astype(np.uint16)


def unstriped8(offs):
    return offs.reshape(8, 16, -1).transpose(0, 2, 1).reshape(8, -1).astype(np.int64)


def pick8(x, idx, run):
    r = np.arange(len(x))
    return x[r[:, None], idx[r % (8 * run) // run]]


E2M1 = np.array([0.0, 0.5, 1.0, 1.5, 2.0, 3.0, 4.0, 6.0, -0.0, -0.5, -1.0, -1.5, -2.0, -3.0, -4.0, -6.0])


def pack_weight(w, fmt):
    k, n = w.shape
    w = f64(np.asarray(w, np.float32).astype(ml_dtypes.bfloat16)).reshape(k // 32, 32, n)
    amax = np.abs(w).max(1)
    if fmt == "e4m3":
        byte = np.frexp(amax)[1] - 1 + 127 - 7
    else:
        mant, ex = np.frexp(amax / 6.0)
        byte = np.where(mant > 0.5, ex, ex - 1) + 127
    byte = np.clip(np.where(amax > 0, byte, 1), 1, 254)
    scaled = (w * np.exp2(127.0 - byte)[:, None, :]).reshape(k, n).astype(np.float32)
    by_word = np.ascontiguousarray(scaled.reshape(k // 512, 128, 4, n).transpose(0, 1, 3, 2))
    if fmt == "e4m3":
        words = by_word.astype(ml_dtypes.float8_e4m3fn).view(np.uint8)
    else:
        c = by_word.astype(ml_dtypes.float4_e2m1fn).view(np.uint8) & 0xF
        words = (c[..., 0::2] | (c[..., 1::2] << 4)).reshape(k // 512, 128, 2 * n)
    return np.ascontiguousarray(words), np.ascontiguousarray(byte.astype(np.uint8).reshape(k // 512, 16, n))


def unpack_weight(words, scales, fmt):
    g, _, n = scales.shape
    words = np.ascontiguousarray(words).reshape(g, 128, n, -1)
    if fmt == "e4m3":
        vals = words.view(ml_dtypes.float8_e4m3fn).astype(np.float64)
    else:
        nib = np.empty((g, 128, n, 4), np.uint8)
        nib[..., 0::2] = words & 0xF
        nib[..., 1::2] = words >> 4
        vals = E2M1[nib]
    vals = vals * np.repeat(np.exp2(scales.astype(np.float64) - 127.0), 8, axis=1)[..., None]
    return vals.transpose(0, 1, 3, 2).reshape(g * 512, n)


D, T, I, Q = 512, 1024, 512, 128


def setup_inputs():
    n = np.random.standard_normal
    idx = np.stack([np.random.permutation(T)[:I] for _ in range(8)])
    idx2 = np.stack([np.random.permutation(T)[:I] for _ in range(8)])
    idx3 = np.stack([np.random.permutation(T)[:I] for _ in range(8)])
    idx4 = np.stack([np.random.permutation(T)[:I] for _ in range(8)])
    fd = mx_kscale(D)
    keysp = pack_weight(n((D, T)) / fd[:, None], "e2m1")
    return {
        "query": (n((D, Q)) * 0.9 / np.sqrt(D) * fd[:, None]).astype(np.float32),
        "keys_words": keysp[0],
        "keys_scales": keysp[1],
        "lam": (np.random.uniform(0.3, 0.9, (Q, 1))).astype(np.float32),
        "reserve": (np.random.uniform(0.5, 2.0, (Q, 1))).astype(np.float32),
        "old": (np.random.uniform(0.0, 2.0, (Q, T))).astype(np.float32),
        "gainm": (np.random.uniform(0.5, 1.5, (Q, I))).astype(np.float32),
        "offs": striped8(idx),
        "offs2": striped8(idx2),
        "offs3": striped8(idx3),
        "offs4": striped8(idx4),
    }


def reference(query, keys_words, keys_scales, lam, reserve, old, gainm, offs, offs2, offs3, offs4):
    idx = unstriped8(offs)
    idx2 = unstriped8(offs2)
    idx3 = unstriped8(offs3)
    idx4 = unstriped8(offs4)
    keysu = unpack_weight(keys_words, keys_scales, "e2m1")
    queryq = mxq(f64(query), 0, "e4m3")
    a = queryq.T @ keysu
    s = pick8(a, idx, 16) + np.maximum(pick8(a, idx2, 16), pick8(a, idx3, 16)) * f64(lam)
    p = np.exp(s - np.max(s, axis=1, keepdims=True))
    r = p / np.sum(p, axis=1, keepdims=True)
    u0 = r * np.log(r) * (-1.0)
    w = u0 / (np.sum(u0, axis=1, keepdims=True) + f64(reserve))
    ws = w * f64(gainm) * 512.0
    wf = np.zeros((Q, T))
    wf[np.arange(Q)[:, None], idx4[np.arange(Q) % 128 // 16]] = ws
    y = f64(old) + wf
    return y

@@ -1,0 +1,187 @@
+import math
+from contextlib import ExitStack
+
+import concourse.mybir as mybir
+
+D, T, I, Q = 512, 1024, 512, 128
+FLOPS = 2 * D * T * Q
+
+F32 = mybir.dt.float32
+BF16 = mybir.dt.bfloat16
+I32 = mybir.dt.int32
+U32 = mybir.dt.uint32
+U16 = mybir.dt.uint16
+U8 = mybir.dt.uint8
+FP8X4 = mybir.dt.float8_e4m3fn_x4
+FP4X4 = mybir.dt.float4_e2m1fn_x4
+ALU = mybir.AluOpType
+ACT = mybir.ActivationFunctionType
+
+P = 128
+PACK = 4
+SCORE_WIDTHS = (256, 256, 256, 128, 128)
+HALF = I // 2
+OUT_WIDTHS = (128, 256, 256, 256, 128)
+
+LOG_SLOPE = math.log(2.0) / 2.0**23
+LOG_SHIFT = 88.0
+
+
+def tile_attend_lookahead_lacking_moved_heads_kernel(
+    tc, query, keys_words, keys_scales, lam, reserve, old, gainm, offs, offs2, offs3, offs4, out
+):
+    nc = tc.nc
+    with ExitStack() as ctx:
+        pool = ctx.enter_context(tc.tile_pool(name="keep", bufs=1))
+        psum = ctx.enter_context(tc.psum_pool(name="psum", bufs=1))
+
+        def column(name):
+            return pool.tile([P, 1], F32, name=name)
+
+        q_raw = pool.tile([P, PACK, Q], F32)
+        nc.sync.dma_start(out=q_raw[:], in_=query.rearrange("(p j) q -> p j q", j=PACK))
+        k_words = pool.tile([P, 2 * T], U8, align_bytes=64)
+        nc.sync.dma_start(out=k_words[:].bitcast(I32), in_=keys_words[0].bitcast(I32))
+        k_scales = pool.tile([P, T], U8, align_bytes=64)
+        nc.vector.memset(k_scales[:].bitcast(I32), 0)
+        for quad in range(4):
+            nc.scalar.dma_start(
+                out=k_scales[32 * quad : 32 * quad + 4, :].bitcast(I32),
+                in_=keys_scales[0, 4 * quad : 4 * quad + 4, :].bitcast(I32),
+            )
+        list2 = pool.tile([P, I // 16], U16)
+        nc.sync.dma_start(list2[:], offs2)
+        list3 = pool.tile([P, I // 16], U16)
+        nc.sync.dma_start(list3[:], offs3)
+        list1 = pool.tile([P, I // 16], U16)
+        nc.sync.dma_start(list1[:], offs)
+        lam_col = column("lam_col")
+        nc.gpsimd.dma_start(out=lam_col[:], in_=lam)
+        reserve_col = column("reserve_col")
+        nc.gpsimd.dma_start(out=reserve_col[:], in_=reserve)
+        gain = pool.tile([P, I], F32)
+        nc.sync.dma_start(out=gain[:], in_=gainm)
+        list4 = pool.tile([P, I // 16], U16)
+        nc.sync.dma_start(list4[:], offs4)
+        counts = pool.tile([P, T], F32)
+        nc.sync.dma_start(out=counts[:], in_=old)
+        placed = pool.tile([P, T], F32)
+        nc.vector.memset(placed[:], 0.0)
+        shifts = pool.tile([P, 4], F32)
+        for step in range(4):
+            nc.vector.memset(shifts[:, step : step + 1], LOG_SHIFT + step)
+
+        q_grouped = pool.tile([P, Q, PACK], BF16, align_bytes=64)
+        nc.vector.tensor_copy(out=q_grouped[:], in_=q_raw[:].rearrange("p j q -> p q j"))
+        q_codes = pool.tile([P, Q], U32, align_bytes=64)
+        q_scales = pool.tile([P, Q], U8, align_bytes=64)
+        nc.vector.quantize_mx(
+            out=q_codes[:].bitcast(FP8X4), scales=q_scales[:], in_=q_grouped[:].rearrange("p q j -> p (q j)")
+        )
+
+        a = pool.tile([P, T], F32)
+        start = 0
+        for n, width in enumerate(SCORE_WIDTHS):
+            cols = slice(start, start + width)
+            bank = psum.tile([P, width], F32, name=f"bank{n}")
+            nc.tensor.matmul_mx(
+                out=bank[:],
+                lhsT=q_codes[:].bitcast(FP8X4),
+                lhsT_scale=q_scales[:],
+                rhs=k_words[:, 2 * start : 2 * (start + width)].bitcast(FP4X4),
+                rhs_scale=k_scales[:, cols],
+                start=True,
+                stop=True,
+            )
+            if n % 2 == 0:
+                nc.scalar.copy(out=a[:, cols], in_=bank[:])
+            else:
+                nc.vector.tensor_copy(out=a[:, cols], in_=bank[:])
+            start = start + width
+
+        halves = [slice(h * HALF, (h + 1) * HALF) for h in range(2)]
+        list_halves = [slice(h * HALF // 16, (h + 1) * HALF // 16) for h in range(2)]
+        first = pool.tile([P, I], F32)
+        second = pool.tile([P, I], F32)
+        third = pool.tile([P, I], F32)
+        for h in range(2):
+            nc.vector.tensor_copy(second[:, halves[h]], a[:].indirect(list2[:, list_halves[h]]))
+            nc.scalar.activation(third[:, halves[h]], a[:].indirect(list3[:, list_halves[h]]), ACT.Copy)
+            nc.scalar.activation(first[:, halves[h]], a[:].indirect(list1[:, list_halves[h]]), ACT.Copy)
+        larger = pool.tile([P, I], F32)
+        s = pool.tile([P, I], F32)
+        neg_s = pool.tile([P, I], F32)
+        neg_max_part = column("neg_max_part")
+        neg_max = column("neg_max")
+
+        def take_larger(h):
+            nc.vector.tensor_tensor(larger[:, halves[h]], second[:, halves[h]], third[:, halves[h]], ALU.max)
+
+        def score(h):
+            nc.vector.scalar_tensor_tensor(
+                s[:, halves[h]], larger[:, halves[h]], lam_col[:], first[:, halves[h]], ALU.mult, ALU.add
+            )
+
+        def negate_and_reduce(h, least_so_far, least):
+            nc.vector.tensor_scalar(
+                neg_s[:, halves[h]], s[:, halves[h]], -1.0, least_so_far, ALU.mult, ALU.min, accum_out=least[:]
+            )
+
+        take_larger(0)
+        score(0)
+        take_larger(1)
+        negate_and_reduce(0, None, neg_max_part)
+        score(1)
+        negate_and_reduce(1, neg_max_part[:], neg_max)
+
+        p = pool.tile([P, I], F32)
+        z = column("z")
+        nc.scalar.activation(p[:], s[:], ACT.Exp, bias=neg_max[:], accum_out=z[:])
+        gap = pool.tile([P, I], F32)
+        nc.vector.tensor_scalar(gap[:], neg_s[:], neg_max[:], None, ALU.subtract)
+
+        z_bits = z[:].bitcast(U32)
+        exp_neg_y = column("exp_neg_y0")
+        nc.scalar.activation(exp_neg_y[:], z_bits, ACT.Exp, scale=-LOG_SLOPE, bias=shifts[:, 0:1])
+        neg_z = column("neg_z")
+        nc.scalar.activation(neg_z[:], z[:], ACT.Copy, scale=-1.0)
+        less_y = []
+        for c in (1, 2, 3):
+            col = column(f"less_y0_{c}")
+            nc.scalar.activation(col[:], z_bits, ACT.Identity, scale=-LOG_SLOPE, bias=shifts[:, c : c + 1])
+            less_y.append(col)
+        for step in (1, 2):
+            next_exp = column(f"exp_neg_y{step}")
+            nc.scalar.activation(next_exp[:], exp_neg_y[:], ACT.Exp, scale=neg_z[:], bias=less_y[0][:])
+            next_less = []
+            for c in range(1, len(less_y)):
+                col = column(f"less_y{step}_{c}")
+                nc.scalar.activation(col[:], exp_neg_y[:], ACT.Identity, scale=neg_z[:], bias=less_y[c][:])
+                next_less.append(col)
+            exp_neg_y, less_y = next_exp, next_less
+        neg_log_z = column("neg_log_z")
+        nc.scalar.activation(neg_log_z[:], exp_neg_y[:], ACT.Identity, scale=neg_z[:], bias=less_y[0][:])
+
+        p_gap = pool.tile([P, I], F32)
+        p_gap_sum = column("p_gap_sum")
+        nc.vector.scalar_tensor_tensor(p_gap[:], gap[:], 1.0, p[:], ALU.mult, ALU.mult, accum_out=p_gap_sum[:])
+        p_gain = pool.tile([P, I], F32)
+        nc.vector.scalar_tensor_tensor(p_gain[:], p[:], 512.0, gain[:], ALU.mult, ALU.mult)
+        rest = column("rest")
+        nc.vector.tensor_scalar(rest[:], z[:], reserve_col[:], p_gap_sum[:], ALU.mult, ALU.add)
+        denom = column("denom")
+        nc.vector.tensor_scalar(denom[:], neg_log_z[:], neg_z[:], rest[:], ALU.mult, ALU.add)
+        inv = column("inv")
+        nc.vector.reciprocal(inv[:], denom[:])
+        share = pool.tile([P, I], F32)
+        nc.vector.tensor_scalar(share[:], gap[:], neg_log_z[:], inv[:], ALU.subtract, ALU.mult)
+        nc.vector.tensor_tensor(placed[:].indirect(list4[:]), share[:], p_gain[:], ALU.mult)
+
+        start = 0
+        for n, width in enumerate(OUT_WIDTHS):
+            cols = slice(start, start + width)
+            result = pool.tile([P, width], F32, name=f"result{n}")
+            nc.vector.tensor_tensor(result[:], placed[:, cols], counts[:, cols], ALU.add)
+            queue = nc.sync if n % 2 == 0 else nc.scalar
+            queue.dma_start(out=out[:, cols], in_=result[:])
+            start = start + width

@@ -25,6 +25,7 @@ OUT_WIDTHS = (128, 256, 256, 256, 128)
 
 LOG_SLOPE = math.log(2.0) / 2.0**23
 LOG_SHIFT = 88.0
+LOG_TERMS = 12
 
 
 def tile_attend_lookahead_lacking_moved_heads_kernel(
@@ -56,28 +57,42 @@ def tile_attend_lookahead_lacking_moved_heads_kernel(
         list1 = pool.tile([P, I // 16], U16)
         nc.sync.dma_start(list1[:], offs)
         lam_col = column("lam_col")
-        nc.gpsimd.dma_start(out=lam_col[:], in_=lam)
-        reserve_col = column("reserve_col")
-        nc.gpsimd.dma_start(out=reserve_col[:], in_=reserve)
+        nc.sync.dma_start(out=lam_col[:], in_=lam)
         gain = pool.tile([P, I], F32)
         nc.sync.dma_start(out=gain[:], in_=gainm)
         list4 = pool.tile([P, I // 16], U16)
         nc.sync.dma_start(list4[:], offs4)
+        reserve_col = column("reserve_col")
+        nc.sync.dma_start(out=reserve_col[:], in_=reserve)
         counts = pool.tile([P, T], F32)
         nc.sync.dma_start(out=counts[:], in_=old)
         placed = pool.tile([P, T], F32)
         nc.vector.memset(placed[:], 0.0)
-        shifts = pool.tile([P, 4], F32)
-        for step in range(4):
-            nc.vector.memset(shifts[:, step : step + 1], LOG_SHIFT + step)
+        shift = column("shift")
+        nc.vector.memset(shift[:], LOG_SHIFT)
+        neg_shift = column("neg_shift")
+        nc.vector.memset(neg_shift[:], -LOG_SHIFT)
+        factors = pool.tile([P, LOG_TERMS + 3], F32)
+        addends = pool.tile([P, LOG_TERMS + 3], F32)
+        orders = pool.tile([P, LOG_TERMS], F32)
+        nc.gpsimd.iota(
+            orders[:], [[1, LOG_TERMS]], base=-LOG_TERMS, channel_multiplier=0, allow_small_or_imprecise_dtypes=True
+        )
+        nc.vector.reciprocal(addends[:, :LOG_TERMS], orders[:])
+        nc.vector.memset(factors[:, LOG_TERMS + 2 :], 1.0)
 
         q_grouped = pool.tile([P, Q, PACK], BF16, align_bytes=64)
-        nc.vector.tensor_copy(out=q_grouped[:], in_=q_raw[:].rearrange("p j q -> p q j"))
         q_codes = pool.tile([P, Q], U32, align_bytes=64)
         q_scales = pool.tile([P, Q], U8, align_bytes=64)
-        nc.vector.quantize_mx(
-            out=q_codes[:].bitcast(FP8X4), scales=q_scales[:], in_=q_grouped[:].rearrange("p q j -> p (q j)")
-        )
+        q_halves = [slice(h * Q // 2, (h + 1) * Q // 2) for h in range(2)]
+        for rows in q_halves:
+            nc.vector.tensor_copy(out=q_grouped[:, rows, :], in_=q_raw[:, :, rows].rearrange("p j q -> p q j"))
+        for rows in q_halves:
+            nc.vector.quantize_mx(
+                out=q_codes[:, rows].bitcast(FP8X4),
+                scales=q_scales[:, rows],
+                in_=q_grouped[:, rows, :].rearrange("p q j -> p (q j)"),
+            )
 
         a = pool.tile([P, T], F32)
         start = 0
@@ -135,46 +150,48 @@ def tile_attend_lookahead_lacking_moved_heads_kernel(
         negate_and_reduce(1, neg_max_part[:], neg_max)
 
         p = pool.tile([P, I], F32)
-        z = column("z")
-        nc.scalar.activation(p[:], s[:], ACT.Exp, bias=neg_max[:], accum_out=z[:])
+        z = factors[:, LOG_TERMS + 1 : LOG_TERMS + 2]
+        nc.scalar.activation(p[:], s[:], ACT.Exp, bias=neg_max[:], accum_out=z)
         gap = pool.tile([P, I], F32)
         nc.vector.tensor_scalar(gap[:], neg_s[:], neg_max[:], None, ALU.subtract)
 
-        z_bits = z[:].bitcast(U32)
-        exp_neg_y = column("exp_neg_y0")
-        nc.scalar.activation(exp_neg_y[:], z_bits, ACT.Exp, scale=-LOG_SLOPE, bias=shifts[:, 0:1])
+        z_bits = z.bitcast(U32)
+        exp_neg_guess = column("exp_neg_guess")
+        nc.scalar.activation(exp_neg_guess[:], z_bits, ACT.Exp, scale=-LOG_SLOPE, bias=shift[:])
         neg_z = column("neg_z")
-        nc.scalar.activation(neg_z[:], z[:], ACT.Copy, scale=-1.0)
-        less_y = []
-        for c in (1, 2, 3):
-            col = column(f"less_y0_{c}")
-            nc.scalar.activation(col[:], z_bits, ACT.Identity, scale=-LOG_SLOPE, bias=shifts[:, c : c + 1])
-            less_y.append(col)
-        for step in (1, 2):
-            next_exp = column(f"exp_neg_y{step}")
-            nc.scalar.activation(next_exp[:], exp_neg_y[:], ACT.Exp, scale=neg_z[:], bias=less_y[0][:])
-            next_less = []
-            for c in range(1, len(less_y)):
-                col = column(f"less_y{step}_{c}")
-                nc.scalar.activation(col[:], exp_neg_y[:], ACT.Identity, scale=neg_z[:], bias=less_y[c][:])
-                next_less.append(col)
-            exp_neg_y, less_y = next_exp, next_less
-        neg_log_z = column("neg_log_z")
-        nc.scalar.activation(neg_log_z[:], exp_neg_y[:], ACT.Identity, scale=neg_z[:], bias=less_y[0][:])
+        nc.scalar.activation(neg_z[:], z, ACT.Copy, scale=-1.0)
+        nc.scalar.activation(
+            addends[:, LOG_TERMS : LOG_TERMS + 1], z_bits, ACT.Identity, scale=LOG_SLOPE, bias=neg_shift[:]
+        )
+        nc.scalar.activation(addends[:, LOG_TERMS + 1 : LOG_TERMS + 2], reserve_col[:], ACT.Copy, scale=z)
+        nc.scalar.activation(
+            factors[:, : LOG_TERMS + 1],
+            exp_neg_guess[:].to_broadcast([P, LOG_TERMS + 1]),
+            ACT.Identity,
+            scale=neg_z[:],
+            bias=1.0,
+        )
 
         p_gap = pool.tile([P, I], F32)
-        p_gap_sum = column("p_gap_sum")
-        nc.vector.scalar_tensor_tensor(p_gap[:], gap[:], 1.0, p[:], ALU.mult, ALU.mult, accum_out=p_gap_sum[:])
+        nc.vector.scalar_tensor_tensor(
+            p_gap[:], gap[:], 1.0, p[:], ALU.mult, ALU.mult, accum_out=addends[:, LOG_TERMS + 2 :]
+        )
         p_gain = pool.tile([P, I], F32)
-        nc.vector.scalar_tensor_tensor(p_gain[:], p[:], 512.0, gain[:], ALU.mult, ALU.mult)
-        rest = column("rest")
-        nc.vector.tensor_scalar(rest[:], z[:], reserve_col[:], p_gap_sum[:], ALU.mult, ALU.add)
-        denom = column("denom")
-        nc.vector.tensor_scalar(denom[:], neg_log_z[:], neg_z[:], rest[:], ALU.mult, ALU.add)
+
+        def weigh(h):
+            nc.vector.scalar_tensor_tensor(
+                p_gain[:, halves[h]], p[:, halves[h]], 512.0, gain[:, halves[h]], ALU.mult, ALU.mult
+            )
+
+        weigh(0)
+        chain = pool.tile([P, LOG_TERMS + 3], F32)
+        nc.vector.tensor_tensor_scan(chain[:], factors[:], addends[:], 0.0, ALU.mult, ALU.add)
+        weigh(1)
+        log_z = chain[:, LOG_TERMS : LOG_TERMS + 1]
         inv = column("inv")
-        nc.vector.reciprocal(inv[:], denom[:])
+        nc.vector.reciprocal(inv[:], chain[:, LOG_TERMS + 2 :])
         share = pool.tile([P, I], F32)
-        nc.vector.tensor_scalar(share[:], gap[:], neg_log_z[:], inv[:], ALU.subtract, ALU.mult)
+        nc.vector.tensor_scalar(share[:], gap[:], log_z, inv[:], ALU.add, ALU.mult)
         nc.vector.tensor_tensor(placed[:].indirect(list4[:]), share[:], p_gain[:], ALU.mult)
 
         start = 0

@@ -21,7 +21,7 @@ P = 128
 PACK = 4
 SCORE_WIDTHS = (256, 256, 256, 128, 128)
 HALF = I // 2
-OUT_WIDTHS = (128, 256, 256, 256, 128)
+OUT_WIDTHS = (256, 320, 320, 128)
 
 LOG_SLOPE = math.log(2.0) / 2.0**23
 LOG_SHIFT = 88.0
@@ -72,14 +72,16 @@ def tile_attend_lookahead_lacking_moved_heads_kernel(
         nc.vector.memset(shift[:], LOG_SHIFT)
         neg_shift = column("neg_shift")
         nc.vector.memset(neg_shift[:], -LOG_SHIFT)
-        factors = pool.tile([P, LOG_TERMS + 3], F32)
-        addends = pool.tile([P, LOG_TERMS + 3], F32)
+        factors = pool.tile([P, LOG_TERMS + 4], F32)
+        addends = pool.tile([P, LOG_TERMS + 4], F32)
         orders = pool.tile([P, LOG_TERMS], F32)
         nc.gpsimd.iota(
             orders[:], [[1, LOG_TERMS]], base=-LOG_TERMS, channel_multiplier=0, allow_small_or_imprecise_dtypes=True
         )
         nc.vector.reciprocal(addends[:, :LOG_TERMS], orders[:])
-        nc.vector.memset(factors[:, LOG_TERMS + 2 :], 1.0)
+        nc.vector.memset(factors[:, LOG_TERMS + 2 : LOG_TERMS + 3], 1.0)
+        nc.vector.memset(factors[:, LOG_TERMS + 3 :], 1.0 / 512.0)
+        nc.vector.memset(addends[:, LOG_TERMS + 3 :], 0.0)
 
         q_grouped = pool.tile([P, Q, PACK], BF16, align_bytes=64)
         q_codes = pool.tile([P, Q], U32, align_bytes=64)
@@ -142,28 +144,48 @@ def tile_attend_lookahead_lacking_moved_heads_kernel(
                 neg_s[:, halves[h]], s[:, halves[h]], -1.0, least_so_far, ALU.mult, ALU.min, accum_out=least[:]
             )
 
+        p = pool.tile([P, I], F32)
+        z_part = column("z_part")
+        z_rest = column("z_rest")
         take_larger(0)
         score(0)
         take_larger(1)
         negate_and_reduce(0, None, neg_max_part)
+        nc.scalar.activation(p[:, halves[0]], s[:, halves[0]], ACT.Exp, bias=neg_max_part[:], accum_out=z_part[:])
         score(1)
         negate_and_reduce(1, neg_max_part[:], neg_max)
+        rescale = column("rescale")
+        nc.scalar.activation(rescale[:], neg_max_part[:], ACT.Exp, scale=-1.0, bias=neg_max[:])
+        nc.scalar.activation(p[:, halves[1]], s[:, halves[1]], ACT.Exp, bias=neg_max[:], accum_out=z_rest[:])
 
-        p = pool.tile([P, I], F32)
+        p_gap = pool.tile([P, I], F32)
+        p_gap_part = column("p_gap_part")
+        p_gain = pool.tile([P, I], F32)
+
+        def sum_p_gap(h, total):
+            nc.vector.scalar_tensor_tensor(
+                p_gap[:, halves[h]], neg_s[:, halves[h]], neg_max[:], p[:, halves[h]], ALU.subtract, ALU.mult,
+                accum_out=total,
+            )
+
+        sum_p_gap(0, p_gap_part[:])
+        nc.vector.scalar_tensor_tensor(
+            p_gain[:, halves[0]], p[:, halves[0]], rescale[:], gain[:, halves[0]], ALU.mult, ALU.mult
+        )
+        sum_p_gap(1, addends[:, LOG_TERMS + 2 : LOG_TERMS + 3])
+
         z = factors[:, LOG_TERMS + 1 : LOG_TERMS + 2]
-        nc.scalar.activation(p[:], s[:], ACT.Exp, bias=neg_max[:], accum_out=z)
-        gap = pool.tile([P, I], F32)
-        nc.vector.tensor_scalar(gap[:], neg_s[:], neg_max[:], None, ALU.subtract)
-
+        nc.scalar.activation(z, z_part[:], ACT.Identity, scale=rescale[:], bias=z_rest[:])
         z_bits = z.bitcast(U32)
         exp_neg_guess = column("exp_neg_guess")
         nc.scalar.activation(exp_neg_guess[:], z_bits, ACT.Exp, scale=-LOG_SLOPE, bias=shift[:])
         neg_z = column("neg_z")
         nc.scalar.activation(neg_z[:], z, ACT.Copy, scale=-1.0)
+        z_reserve = column("z_reserve")
+        nc.scalar.activation(z_reserve[:], reserve_col[:], ACT.Copy, scale=z)
         nc.scalar.activation(
             addends[:, LOG_TERMS : LOG_TERMS + 1], z_bits, ACT.Identity, scale=LOG_SLOPE, bias=neg_shift[:]
         )
-        nc.scalar.activation(addends[:, LOG_TERMS + 1 : LOG_TERMS + 2], reserve_col[:], ACT.Copy, scale=z)
         nc.scalar.activation(
             factors[:, : LOG_TERMS + 1],
             exp_neg_guess[:].to_broadcast([P, LOG_TERMS + 1]),
@@ -171,27 +193,20 @@ def tile_attend_lookahead_lacking_moved_heads_kernel(
             scale=neg_z[:],
             bias=1.0,
         )
-
-        p_gap = pool.tile([P, I], F32)
-        nc.vector.scalar_tensor_tensor(
-            p_gap[:], gap[:], 1.0, p[:], ALU.mult, ALU.mult, accum_out=addends[:, LOG_TERMS + 2 :]
+        nc.scalar.activation(
+            addends[:, LOG_TERMS + 1 : LOG_TERMS + 2], p_gap_part[:], ACT.Identity, scale=rescale[:], bias=z_reserve[:]
         )
-        p_gain = pool.tile([P, I], F32)
 
-        def weigh(h):
-            nc.vector.scalar_tensor_tensor(
-                p_gain[:, halves[h]], p[:, halves[h]], 512.0, gain[:, halves[h]], ALU.mult, ALU.mult
-            )
-
-        weigh(0)
-        chain = pool.tile([P, LOG_TERMS + 3], F32)
+        nc.vector.tensor_tensor(p_gain[:, halves[1]], p[:, halves[1]], gain[:, halves[1]], ALU.mult)
+        chain = pool.tile([P, LOG_TERMS + 4], F32)
         nc.vector.tensor_tensor_scan(chain[:], factors[:], addends[:], 0.0, ALU.mult, ALU.add)
-        weigh(1)
         log_z = chain[:, LOG_TERMS : LOG_TERMS + 1]
         inv = column("inv")
-        nc.vector.reciprocal(inv[:], chain[:, LOG_TERMS + 2 :])
+        nc.vector.reciprocal(inv[:], chain[:, LOG_TERMS + 3 :])
+        log_sum = column("log_sum")
+        nc.vector.tensor_scalar(log_sum[:], log_z, neg_max[:], None, ALU.subtract)
         share = pool.tile([P, I], F32)
-        nc.vector.tensor_scalar(share[:], gap[:], log_z, inv[:], ALU.add, ALU.mult)
+        nc.vector.tensor_scalar(share[:], neg_s[:], log_sum[:], inv[:], ALU.add, ALU.mult)
         nc.vector.tensor_tensor(placed[:].indirect(list4[:]), share[:], p_gain[:], ALU.mult)
 
         start = 0

import math
from contextlib import ExitStack

import concourse.mybir as mybir

D, T, I, Q = 512, 1024, 512, 128
FLOPS = 2 * D * T * Q

F32 = mybir.dt.float32
BF16 = mybir.dt.bfloat16
I32 = mybir.dt.int32
U32 = mybir.dt.uint32
U16 = mybir.dt.uint16
U8 = mybir.dt.uint8
FP8X4 = mybir.dt.float8_e4m3fn_x4
FP4X4 = mybir.dt.float4_e2m1fn_x4
ALU = mybir.AluOpType
ACT = mybir.ActivationFunctionType

P = 128
PACK = 4
SCORE_WIDTHS = (256, 256, 256, 128, 128)
HALF = I // 2
OUT_WIDTHS = (256, 320, 320, 128)

LOG_SLOPE = math.log(2.0) / 2.0**23
LOG_SHIFT = 88.0
LOG_TERMS = 12


def tile_attend_lookahead_lacking_moved_heads_kernel(
    tc, query, keys_words, keys_scales, lam, reserve, old, gainm, offs, offs2, offs3, offs4, out
):
    nc = tc.nc
    with ExitStack() as ctx:
        pool = ctx.enter_context(tc.tile_pool(name="keep", bufs=1))
        psum = ctx.enter_context(tc.psum_pool(name="psum", bufs=1))

        def column(name):
            return pool.tile([P, 1], F32, name=name)

        q_raw = pool.tile([P, PACK, Q], F32)
        nc.sync.dma_start(out=q_raw[:], in_=query.rearrange("(p j) q -> p j q", j=PACK))
        k_words = pool.tile([P, 2 * T], U8, align_bytes=64)
        nc.sync.dma_start(out=k_words[:].bitcast(I32), in_=keys_words[0].bitcast(I32))
        k_scales = pool.tile([P, T], U8, align_bytes=64)
        nc.vector.memset(k_scales[:].bitcast(I32), 0)
        for quad in range(4):
            nc.scalar.dma_start(
                out=k_scales[32 * quad : 32 * quad + 4, :].bitcast(I32),
                in_=keys_scales[0, 4 * quad : 4 * quad + 4, :].bitcast(I32),
            )
        list2 = pool.tile([P, I // 16], U16)
        nc.sync.dma_start(list2[:], offs2)
        list3 = pool.tile([P, I // 16], U16)
        nc.sync.dma_start(list3[:], offs3)
        list1 = pool.tile([P, I // 16], U16)
        nc.sync.dma_start(list1[:], offs)
        lam_col = column("lam_col")
        nc.sync.dma_start(out=lam_col[:], in_=lam)
        gain = pool.tile([P, I], F32)
        nc.sync.dma_start(out=gain[:], in_=gainm)
        list4 = pool.tile([P, I // 16], U16)
        nc.sync.dma_start(list4[:], offs4)
        reserve_col = column("reserve_col")
        nc.sync.dma_start(out=reserve_col[:], in_=reserve)
        counts = pool.tile([P, T], F32)
        nc.sync.dma_start(out=counts[:], in_=old)
        placed = pool.tile([P, T], F32)
        nc.vector.memset(placed[:], 0.0)
        shift = column("shift")
        nc.vector.memset(shift[:], LOG_SHIFT)
        neg_shift = column("neg_shift")
        nc.vector.memset(neg_shift[:], -LOG_SHIFT)
        factors = pool.tile([P, LOG_TERMS + 4], F32)
        addends = pool.tile([P, LOG_TERMS + 4], F32)
        orders = pool.tile([P, LOG_TERMS], F32)
        nc.gpsimd.iota(
            orders[:], [[1, LOG_TERMS]], base=-LOG_TERMS, channel_multiplier=0, allow_small_or_imprecise_dtypes=True
        )
        nc.vector.reciprocal(addends[:, :LOG_TERMS], orders[:])
        nc.vector.memset(factors[:, LOG_TERMS + 2 : LOG_TERMS + 3], 1.0)
        nc.vector.memset(factors[:, LOG_TERMS + 3 :], 1.0 / 512.0)
        nc.vector.memset(addends[:, LOG_TERMS + 3 :], 0.0)

        q_grouped = pool.tile([P, Q, PACK], BF16, align_bytes=64)
        q_codes = pool.tile([P, Q], U32, align_bytes=64)
        q_scales = pool.tile([P, Q], U8, align_bytes=64)
        q_halves = [slice(h * Q // 2, (h + 1) * Q // 2) for h in range(2)]
        for rows in q_halves:
            nc.vector.tensor_copy(out=q_grouped[:, rows, :], in_=q_raw[:, :, rows].rearrange("p j q -> p q j"))
        for rows in q_halves:
            nc.vector.quantize_mx(
                out=q_codes[:, rows].bitcast(FP8X4),
                scales=q_scales[:, rows],
                in_=q_grouped[:, rows, :].rearrange("p q j -> p (q j)"),
            )

        a = pool.tile([P, T], F32)
        start = 0
        for n, width in enumerate(SCORE_WIDTHS):
            cols = slice(start, start + width)
            bank = psum.tile([P, width], F32, name=f"bank{n}")
            nc.tensor.matmul_mx(
                out=bank[:],
                lhsT=q_codes[:].bitcast(FP8X4),
                lhsT_scale=q_scales[:],
                rhs=k_words[:, 2 * start : 2 * (start + width)].bitcast(FP4X4),
                rhs_scale=k_scales[:, cols],
                start=True,
                stop=True,
            )
            if n % 2 == 0:
                nc.scalar.copy(out=a[:, cols], in_=bank[:])
            else:
                nc.vector.tensor_copy(out=a[:, cols], in_=bank[:])
            start = start + width

        halves = [slice(h * HALF, (h + 1) * HALF) for h in range(2)]
        list_halves = [slice(h * HALF // 16, (h + 1) * HALF // 16) for h in range(2)]
        first = pool.tile([P, I], F32)
        second = pool.tile([P, I], F32)
        third = pool.tile([P, I], F32)
        for h in range(2):
            nc.vector.tensor_copy(second[:, halves[h]], a[:].indirect(list2[:, list_halves[h]]))
            nc.scalar.activation(third[:, halves[h]], a[:].indirect(list3[:, list_halves[h]]), ACT.Copy)
            nc.scalar.activation(first[:, halves[h]], a[:].indirect(list1[:, list_halves[h]]), ACT.Copy)
        larger = pool.tile([P, I], F32)
        s = pool.tile([P, I], F32)
        neg_s = pool.tile([P, I], F32)
        neg_max_part = column("neg_max_part")
        neg_max = column("neg_max")

        def take_larger(h):
            nc.vector.tensor_tensor(larger[:, halves[h]], second[:, halves[h]], third[:, halves[h]], ALU.max)

        def score(h):
            nc.vector.scalar_tensor_tensor(
                s[:, halves[h]], larger[:, halves[h]], lam_col[:], first[:, halves[h]], ALU.mult, ALU.add
            )

        def negate_and_reduce(h, least_so_far, least):
            nc.vector.tensor_scalar(
                neg_s[:, halves[h]], s[:, halves[h]], -1.0, least_so_far, ALU.mult, ALU.min, accum_out=least[:]
            )

        p = pool.tile([P, I], F32)
        z_part = column("z_part")
        z_rest = column("z_rest")
        take_larger(0)
        score(0)
        take_larger(1)
        negate_and_reduce(0, None, neg_max_part)
        nc.scalar.activation(p[:, halves[0]], s[:, halves[0]], ACT.Exp, bias=neg_max_part[:], accum_out=z_part[:])
        score(1)
        negate_and_reduce(1, neg_max_part[:], neg_max)
        rescale = column("rescale")
        nc.scalar.activation(rescale[:], neg_max_part[:], ACT.Exp, scale=-1.0, bias=neg_max[:])
        nc.scalar.activation(p[:, halves[1]], s[:, halves[1]], ACT.Exp, bias=neg_max[:], accum_out=z_rest[:])

        p_gap = pool.tile([P, I], F32)
        p_gap_part = column("p_gap_part")
        p_gain = pool.tile([P, I], F32)

        def sum_p_gap(h, total):
            nc.vector.scalar_tensor_tensor(
                p_gap[:, halves[h]], neg_s[:, halves[h]], neg_max[:], p[:, halves[h]], ALU.subtract, ALU.mult,
                accum_out=total,
            )

        sum_p_gap(0, p_gap_part[:])
        nc.vector.scalar_tensor_tensor(
            p_gain[:, halves[0]], p[:, halves[0]], rescale[:], gain[:, halves[0]], ALU.mult, ALU.mult
        )
        sum_p_gap(1, addends[:, LOG_TERMS + 2 : LOG_TERMS + 3])

        z = factors[:, LOG_TERMS + 1 : LOG_TERMS + 2]
        nc.scalar.activation(z, z_part[:], ACT.Identity, scale=rescale[:], bias=z_rest[:])
        z_bits = z.bitcast(U32)
        exp_neg_guess = column("exp_neg_guess")
        nc.scalar.activation(exp_neg_guess[:], z_bits, ACT.Exp, scale=-LOG_SLOPE, bias=shift[:])
        neg_z = column("neg_z")
        nc.scalar.activation(neg_z[:], z, ACT.Copy, scale=-1.0)
        z_reserve = column("z_reserve")
        nc.scalar.activation(z_reserve[:], reserve_col[:], ACT.Copy, scale=z)
        nc.scalar.activation(
            addends[:, LOG_TERMS : LOG_TERMS + 1], z_bits, ACT.Identity, scale=LOG_SLOPE, bias=neg_shift[:]
        )
        nc.scalar.activation(
            factors[:, : LOG_TERMS + 1],
            exp_neg_guess[:].to_broadcast([P, LOG_TERMS + 1]),
            ACT.Identity,
            scale=neg_z[:],
            bias=1.0,
        )
        nc.scalar.activation(
            addends[:, LOG_TERMS + 1 : LOG_TERMS + 2], p_gap_part[:], ACT.Identity, scale=rescale[:], bias=z_reserve[:]
        )

        nc.vector.tensor_tensor(p_gain[:, halves[1]], p[:, halves[1]], gain[:, halves[1]], ALU.mult)
        chain = pool.tile([P, LOG_TERMS + 4], F32)
        nc.vector.tensor_tensor_scan(chain[:], factors[:], addends[:], 0.0, ALU.mult, ALU.add)
        log_z = chain[:, LOG_TERMS : LOG_TERMS + 1]
        inv = column("inv")
        nc.vector.reciprocal(inv[:], chain[:, LOG_TERMS + 3 :])
        log_sum = column("log_sum")
        nc.vector.tensor_scalar(log_sum[:], log_z, neg_max[:], None, ALU.subtract)
        share = pool.tile([P, I], F32)
        nc.vector.tensor_scalar(share[:], neg_s[:], log_sum[:], inv[:], ALU.add, ALU.mult)
        nc.vector.tensor_tensor(placed[:].indirect(list4[:]), share[:], p_gain[:], ALU.mult)

        start = 0
        for n, width in enumerate(OUT_WIDTHS):
            cols = slice(start, start + width)
            result = pool.tile([P, width], F32, name=f"result{n}")
            nc.vector.tensor_tensor(result[:], placed[:, cols], counts[:, cols], ALU.add)
            queue = nc.sync if n % 2 == 0 else nc.scalar
            queue.dma_start(out=out[:, cols], in_=result[:])
            start = start + width
